import numpy as np
import ml_dtypes


def mxq(x, axis, fmt="e4m3"):
    dtype, down = {"e4m3": (ml_dtypes.float8_e4m3fn, 7), "e5m2": (ml_dtypes.float8_e5m2, 14)}[fmt]
    v = np.moveaxis(np.asarray(x, np.float32).astype(ml_dtypes.bfloat16).astype(np.float64), axis, -1)
    blocks = v.reshape(v.shape[:-1] + (-1, 32))
    amax = np.abs(blocks).max(-1, keepdims=True)
    byte = np.maximum(np.where(amax > 0, np.frexp(amax)[1] - 1 + 127, 0) - down, 1)
    scale = np.exp2(byte - 127.0)
    codes = (blocks / scale).astype(np.float32).astype(dtype).astype(np.float64)
    return np.moveaxis((codes * scale).reshape(v.shape), -1, axis)


WIDE = False


def mx_kscale(k):
    if not WIDE:
        return np.ones(k)
    levels = np.array([10, -10, 5, -5, 0])
    if k % 512:
        return np.exp2(np.random.permutation(np.resize(levels, k // 32))).repeat(32)
    a = np.empty((k // 512, 16))
    for p in range(k // 512):
        a[p, :8] = np.random.permutation(np.resize(levels, 8))
        for g in range(8):
            far = levels[np.abs(levels - a[p, g]) >= 10]
            a[p, g + 8] = far[np.random.randint(len(far))]
    return np.exp2(a.ravel()).repeat(32)


def f64(x):
    return np.asarray(x).astype(np.float64)


def striped(idx):
    return np.tile(np.asarray(idx).reshape(-1, 16).T, (8, 1)).astype(np.uint16)


def unstriped(offs):
    return offs[:16].T.reshape(-1).astype(np.int64)


G, K, T, D, M = 256, 4, 2048, 512, 256


def setup_inputs():
    n = np.random.standard_normal
    s = mx_kscale(D)[:, None]
    x = n((D, T)) * s
    idx = np.stack([np.random.permutation(T)[:K] for g in range(G)])
    return {
        "xT": x.astype(np.float32),
        "w": (n((D, M)) / np.sqrt(D) / s).astype(np.float32),
        "bias": (n((M, 1)) - 2.0).astype(np.float32),
        "offs": striped(idx.reshape(-1)),
    }


def reference(xT, w, bias, offs):
    x = f64(xT)[:, unstriped(offs)]
    y = (mxq(f64(w), 0, "e4m3").T @ mxq(x, 0, "e4m3")).reshape(M, G, K).max(-1)
    y = y + f64(bias)
    y = np.maximum(y, 0.0)
    return y

@@ -1,0 +1,140 @@
+from contextlib import ExitStack
+
+import concourse.mybir as mybir
+
+G, K, T, D, M = 256, 4, 2048, 512, 256
+FLOPS = 2 * D * M * G * K
+
+P = 128
+PACK = 4
+NH = 2
+HE = G * K // NH
+HG = G // NH
+B = 256
+MB = M // P
+
+F32 = mybir.dt.float32
+BF16 = mybir.dt.bfloat16
+U32 = mybir.dt.uint32
+U16 = mybir.dt.uint16
+U8 = mybir.dt.uint8
+FP8X4 = mybir.dt.float8_e4m3fn_x4
+MAX = mybir.AluOpType.max
+MULT = mybir.AluOpType.mult
+ADD = mybir.AluOpType.add
+RELU = mybir.ActivationFunctionType.Relu
+X = mybir.AxisListType.X
+
+
+def tile_attend_edge_relu_kernel(tc, xT, w, bias, offs, out):
+    nc = tc.nc
+    with ExitStack() as ctx:
+        keep = ctx.enter_context(tc.tile_pool(name="keep", bufs=1))
+        psum = ctx.enter_context(tc.psum_pool(name="psum", bufs=1))
+
+        offsets = keep.tile([P, G * K // 16], U16, name="offsets")
+        nc.sync.dma_start(offsets[:], offs)
+
+        x_rows = xT.rearrange("(p t) c -> p t c", t=PACK)
+        planes = []
+        for t in range(PACK):
+            plane = keep.tile([P, T], F32, name="plane%d" % t, align_bytes=64)
+            nc.sync.dma_start(plane[:], x_rows[:, t, :])
+            planes.append(plane)
+        w_raw = keep.tile([P, PACK, M], F32, name="w_raw", align_bytes=64)
+        nc.sync.dma_start(w_raw[:], w.rearrange("(p t) m -> p t m", t=PACK))
+        bias_sb = []
+        for m in range(MB):
+            b = keep.tile([P, 1], F32, name="bias%d" % m)
+            nc.sync.dma_start(b[:], bias[m * P : (m + 1) * P, :])
+            bias_sb.append(b)
+
+        warm = keep.tile([P, 1], F32, name="warm")
+        nc.gpsimd.memset(warm[:], 0.0)
+        nc.scalar.activation(warm[:], warm[:], RELU)
+
+        g01 = keep.tile([P, 2, G * K], F32, name="g01", align_bytes=64)
+        g23 = keep.tile([P, 2, G * K], F32, name="g23", align_bytes=64)
+        xb = [keep.tile([P, HE, PACK], BF16, name="xb%d" % h, align_bytes=64) for h in range(NH)]
+        codes = [keep.tile([P, HE], U32, name="codes%d" % h, align_bytes=64) for h in range(NH)]
+        scales = [keep.tile([P, HE], U8, name="scales%d" % h, align_bytes=64) for h in range(NH)]
+        wb = keep.tile([P, M, PACK], BF16, name="wb", align_bytes=64)
+        w_codes = keep.tile([P, M], U32, name="w_codes", align_bytes=64)
+        w_scales = keep.tile([P, M], U8, name="w_scales", align_bytes=64)
+
+        def gather(t, first, count):
+            dst = g01 if t < 2 else g23
+            nc.vector.tensor_copy(
+                dst[:, t % 2, first : first + count],
+                planes[t][:].indirect(offsets[:, first // 16 : (first + count) // 16]),
+            )
+
+        def interleave(src, t0, s):
+            h, c = divmod(s * B, HE)
+            nc.scalar.copy(
+                xb[h][:, c : c + B, t0 : t0 + 2],
+                src[:, :, s * B : (s + 1) * B].rearrange("p t n -> p n t"),
+            )
+
+        def quantise(h):
+            nc.vector.quantize_mx(
+                out=codes[h][:].bitcast(FP8X4),
+                scales=scales[h][:],
+                in_=xb[h][:].rearrange("p n t -> p (n t)"),
+            )
+
+        def multiply(h, m):
+            acc = psum.tile([P, HE], F32, name="acc%d%d" % (h, m))
+            nc.tensor.matmul_mx(
+                out=acc[:],
+                lhsT=w_codes[:, m * P : (m + 1) * P].bitcast(FP8X4),
+                lhsT_scale=w_scales[:, m * P : (m + 1) * P],
+                rhs=codes[h][:].bitcast(FP8X4),
+                rhs_scale=scales[h][:],
+                start=True,
+                stop=True,
+            )
+            return acc
+
+        def finish(h, m, acc):
+            best = keep.tile([P, HG], F32, name="best%d%d" % (h, m))
+            res = keep.tile([P, HG], F32, name="res%d%d" % (h, m))
+            nc.vector.tensor_reduce(
+                out=best[:], in_=acc[:].rearrange("p (g j) -> p g j", j=K), axis=X, op=MAX
+            )
+            nc.scalar.activation(res[:], best[:], RELU, bias=bias_sb[m][:, 0:1])
+            nc.sync.dma_start(out[m * P : (m + 1) * P, h * HG : (h + 1) * HG], res[:])
+
+        for t in range(3):
+            for h in range(NH):
+                gather(t, h * HE, HE)
+            if t == 1:
+                for s in range(4):
+                    interleave(g01, 0, s)
+        for q in range(4):
+            nc.gpsimd.tensor_scalar(
+                wb[:, q * 64 : (q + 1) * 64, :],
+                w_raw[:, :, q * 64 : (q + 1) * 64].rearrange("p t m -> p m t"),
+                1.0, 0.0, MULT, ADD,
+            )
+        gather(3, 0, B)
+        interleave(g23, 2, 0)
+        gather(3, B, B)
+        interleave(g23, 2, 1)
+        gather(3, 2 * B, B)
+        interleave(g23, 2, 2)
+        gather(3, 3 * B, B)
+        interleave(g23, 2, 3)
+        quantise(0)
+        nc.vector.quantize_mx(
+            out=w_codes[:].bitcast(FP8X4), scales=w_scales[:], in_=wb[:].rearrange("p m t -> p (m t)")
+        )
+        acc00 = multiply(0, 0)
+        acc01 = multiply(0, 1)
+        quantise(1)
+        finish(0, 0, acc00)
+        acc10 = multiply(1, 0)
+        acc11 = multiply(1, 1)
+        finish(0, 1, acc01)
+        finish(1, 0, acc10)
+        finish(1, 1, acc11)

@@ -7,11 +7,11 @@ FLOPS = 2 * D * M * G * K
 
 P = 128
 PACK = 4
-NH = 2
-HE = G * K // NH
-HG = G // NH
-B = 256
+E = G * K
 MB = M // P
+NV = (384, 384, 256, 256)
+B = 256
+CUTS = [(0, 1280, T), (0, 1280, T), (0, 1280, T), (0, 1024, 1792, T)]
 
 F32 = mybir.dt.float32
 BF16 = mybir.dt.bfloat16
@@ -20,9 +20,8 @@ U16 = mybir.dt.uint16
 U8 = mybir.dt.uint8
 FP8X4 = mybir.dt.float8_e4m3fn_x4
 MAX = mybir.AluOpType.max
-MULT = mybir.AluOpType.mult
-ADD = mybir.AluOpType.add
 RELU = mybir.ActivationFunctionType.Relu
+COPY = mybir.ActivationFunctionType.Copy
 X = mybir.AxisListType.X
 
 
@@ -30,18 +29,21 @@ def tile_attend_edge_relu_kernel(tc, xT, w, bias, offs, out):
     nc = tc.nc
     with ExitStack() as ctx:
         keep = ctx.enter_context(tc.tile_pool(name="keep", bufs=1))
+        shared = ctx.enter_context(tc.tile_pool(name="shared", bufs=1))
         psum = ctx.enter_context(tc.psum_pool(name="psum", bufs=1))
 
-        offsets = keep.tile([P, G * K // 16], U16, name="offsets")
+        offsets = keep.tile([P, E // 16], U16, name="offsets")
         nc.sync.dma_start(offsets[:], offs)
 
         x_rows = xT.rearrange("(p t) c -> p t c", t=PACK)
-        planes = []
+        planes, halves = [], []
         for t in range(PACK):
             plane = keep.tile([P, T], F32, name="plane%d" % t, align_bytes=64)
-            nc.sync.dma_start(plane[:], x_rows[:, t, :])
+            for a, b in zip(CUTS[t], CUTS[t][1:]):
+                nc.sync.dma_start(plane[:, a:b], x_rows[:, t, a:b])
             planes.append(plane)
-        w_raw = keep.tile([P, PACK, M], F32, name="w_raw", align_bytes=64)
+            halves.append(keep.tile([P, T], BF16, name="half%d" % t, align_bytes=64))
+        w_raw = shared.tile([P, PACK, M], F32, name="w_raw", align_bytes=64, offset=0)
         nc.sync.dma_start(w_raw[:], w.rearrange("(p t) m -> p t m", t=PACK))
         bias_sb = []
         for m in range(MB):
@@ -53,88 +55,78 @@ def tile_attend_edge_relu_kernel(tc, xT, w, bias, offs, out):
         nc.gpsimd.memset(warm[:], 0.0)
         nc.scalar.activation(warm[:], warm[:], RELU)
 
-        g01 = keep.tile([P, 2, G * K], F32, name="g01", align_bytes=64)
-        g23 = keep.tile([P, 2, G * K], F32, name="g23", align_bytes=64)
-        xb = [keep.tile([P, HE, PACK], BF16, name="xb%d" % h, align_bytes=64) for h in range(NH)]
-        codes = [keep.tile([P, HE], U32, name="codes%d" % h, align_bytes=64) for h in range(NH)]
-        scales = [keep.tile([P, HE], U8, name="scales%d" % h, align_bytes=64) for h in range(NH)]
+        xb = keep.tile([P, E, PACK], BF16, name="xb", align_bytes=64)
+        codes, scales = {}, {}
         wb = keep.tile([P, M, PACK], BF16, name="wb", align_bytes=64)
         w_codes = keep.tile([P, M], U32, name="w_codes", align_bytes=64)
         w_scales = keep.tile([P, M], U8, name="w_scales", align_bytes=64)
 
-        def gather(t, first, count):
-            dst = g01 if t < 2 else g23
-            nc.vector.tensor_copy(
-                dst[:, t % 2, first : first + count],
-                planes[t][:].indirect(offsets[:, first // 16 : (first + count) // 16]),
-            )
+        def listed(tile, a, b):
+            return tile[:].indirect(offsets[:, a // 16 : b // 16])
 
-        def interleave(src, t0, s):
-            h, c = divmod(s * B, HE)
-            nc.scalar.copy(
-                xb[h][:, c : c + B, t0 : t0 + 2],
-                src[:, :, s * B : (s + 1) * B].rearrange("p t n -> p n t"),
-            )
+        for t in range(PACK):
+            for a, b in zip(CUTS[t], CUTS[t][1:]):
+                nc.vector.tensor_copy(halves[t][:, a:b], planes[t][:, a:b])
+            step = B if t == PACK - 1 else E - NV[t]
+            for a in range(NV[t], E, step):
+                nc.scalar.activation(xb[:, a : a + step, t], listed(halves[t], a, a + step), COPY)
+            nc.vector.tensor_copy(xb[:, 0 : NV[t], t], listed(planes[t], 0, NV[t]))
 
-        def quantise(h):
+        nc.vector.tensor_copy(wb[:], w_raw[:].rearrange("p t m -> p m t"))
+
+        def quantise(a, b):
+            codes[a] = shared.tile([P, b - a], U32, name="codes%d" % a, align_bytes=64, offset=4 * a)
+            scales[a] = keep.tile([P, b - a], U8, name="scales%d" % a, align_bytes=64)
             nc.vector.quantize_mx(
-                out=codes[h][:].bitcast(FP8X4),
-                scales=scales[h][:],
-                in_=xb[h][:].rearrange("p n t -> p (n t)"),
+                out=codes[a][:].bitcast(FP8X4),
+                scales=scales[a][:],
+                in_=xb[:, a:b, :].rearrange("p n t -> p (n t)"),
             )
 
-        def multiply(h, m):
-            acc = psum.tile([P, HE], F32, name="acc%d%d" % (h, m))
+        def multiply(acc, m, a, b):
             nc.tensor.matmul_mx(
-                out=acc[:],
+                out=acc,
                 lhsT=w_codes[:, m * P : (m + 1) * P].bitcast(FP8X4),
                 lhsT_scale=w_scales[:, m * P : (m + 1) * P],
-                rhs=codes[h][:].bitcast(FP8X4),
-                rhs_scale=scales[h][:],
+                rhs=codes[a][:].bitcast(FP8X4),
+                rhs_scale=scales[a][:],
                 start=True,
                 stop=True,
             )
-            return acc
 
-        def finish(h, m, acc):
-            best = keep.tile([P, HG], F32, name="best%d%d" % (h, m))
-            res = keep.tile([P, HG], F32, name="res%d%d" % (h, m))
+        out_blocks = out.rearrange("(b p) g -> p b g", p=P)
+
+        def finish(acc, blocks, a, b):
+            n = (b - a) // K
+            name = "%d_%d" % (a, blocks[0])
+            best = keep.tile([P, len(blocks), n], F32, name="best" + name)
+            res = keep.tile([P, len(blocks), n], F32, name="res" + name)
             nc.vector.tensor_reduce(
-                out=best[:], in_=acc[:].rearrange("p (g j) -> p g j", j=K), axis=X, op=MAX
+                out=best[:].rearrange("p b g -> p (b g)"),
+                in_=acc[:].rearrange("p (g j) -> p g j", j=K), axis=X, op=MAX,
             )
-            nc.scalar.activation(res[:], best[:], RELU, bias=bias_sb[m][:, 0:1])
-            nc.sync.dma_start(out[m * P : (m + 1) * P, h * HG : (h + 1) * HG], res[:])
+            for i, m in enumerate(blocks):
+                nc.scalar.activation(res[:, i, :], best[:, i, :], RELU, bias=bias_sb[m][:, 0:1])
+            nc.sync.dma_start(out_blocks[:, blocks[0] : blocks[-1] + 1, a // K : b // K], res[:])
 
-        for t in range(3):
-            for h in range(NH):
-                gather(t, h * HE, HE)
-            if t == 1:
-                for s in range(4):
-                    interleave(g01, 0, s)
-        for q in range(4):
-            nc.gpsimd.tensor_scalar(
-                wb[:, q * 64 : (q + 1) * 64, :],
-                w_raw[:, :, q * 64 : (q + 1) * 64].rearrange("p t m -> p m t"),
-                1.0, 0.0, MULT, ADD,
-            )
-        gather(3, 0, B)
-        interleave(g23, 2, 0)
-        gather(3, B, B)
-        interleave(g23, 2, 1)
-        gather(3, 2 * B, B)
-        interleave(g23, 2, 2)
-        gather(3, 3 * B, B)
-        interleave(g23, 2, 3)
-        quantise(0)
+        def group(a, b):
+            if b - a == 512:
+                for m in range(MB):
+                    acc = psum.tile([P, 512], F32, name="acc%d_%d" % (a, m))
+                    multiply(acc[:], m, a, b)
+                    finish(acc, [m], a, b)
+            else:
+                acc = psum.tile([P, 512], F32, name="acc%d" % a)
+                for m in range(MB):
+                    multiply(acc[:, m * 256 : (m + 1) * 256], m, a, b)
+                finish(acc, list(range(MB)), a, b)
+
+        quantise(0, 512)
         nc.vector.quantize_mx(
             out=w_codes[:].bitcast(FP8X4), scales=w_scales[:], in_=wb[:].rearrange("p m t -> p (m t)")
         )
-        acc00 = multiply(0, 0)
-        acc01 = multiply(0, 1)
-        quantise(1)
-        finish(0, 0, acc00)
-        acc10 = multiply(1, 0)
-        acc11 = multiply(1, 1)
-        finish(0, 1, acc01)
-        finish(1, 0, acc10)
-        finish(1, 1, acc11)
+        quantise(512, 768)
+        quantise(768, 1024)
+        group(0, 512)
+        group(512, 768)
+        group(768, 1024)

@@ -9,9 +9,9 @@ P = 128
 PACK = 4
 E = G * K
 MB = M // P
-NV = (384, 384, 256, 256)
 B = 256
-CUTS = [(0, 1280, T), (0, 1280, T), (0, 1280, T), (0, 1024, 1792, T)]
+CUTS = (0, 1280, T)
+NV = (384, 384, B, B)
 
 F32 = mybir.dt.float32
 BF16 = mybir.dt.bfloat16
@@ -33,14 +33,15 @@ def tile_attend_edge_relu_kernel(tc, xT, w, bias, offs, out):
         psum = ctx.enter_context(tc.psum_pool(name="psum", bufs=1))
 
         offsets = keep.tile([P, E // 16], U16, name="offsets")
-        nc.sync.dma_start(offsets[:], offs)
 
         x_rows = xT.rearrange("(p t) c -> p t c", t=PACK)
         planes, halves = [], []
         for t in range(PACK):
             plane = keep.tile([P, T], F32, name="plane%d" % t, align_bytes=64)
-            for a, b in zip(CUTS[t], CUTS[t][1:]):
+            for a, b in zip(CUTS, CUTS[1:]):
                 nc.sync.dma_start(plane[:, a:b], x_rows[:, t, a:b])
+            if t == 0:
+                nc.sync.dma_start(offsets[:], offs)
             planes.append(plane)
             halves.append(keep.tile([P, T], BF16, name="half%d" % t, align_bytes=64))
         w_raw = shared.tile([P, PACK, M], F32, name="w_raw", align_bytes=64, offset=0)
@@ -56,7 +57,6 @@ def tile_attend_edge_relu_kernel(tc, xT, w, bias, offs, out):
         nc.scalar.activation(warm[:], warm[:], RELU)
 
         xb = keep.tile([P, E, PACK], BF16, name="xb", align_bytes=64)
-        codes, scales = {}, {}
         wb = keep.tile([P, M, PACK], BF16, name="wb", align_bytes=64)
         w_codes = keep.tile([P, M], U32, name="w_codes", align_bytes=64)
         w_scales = keep.tile([P, M], U8, name="w_scales", align_bytes=64)
@@ -65,68 +65,73 @@ def tile_attend_edge_relu_kernel(tc, xT, w, bias, offs, out):
             return tile[:].indirect(offsets[:, a // 16 : b // 16])
 
         for t in range(PACK):
-            for a, b in zip(CUTS[t], CUTS[t][1:]):
+            for a, b in zip(CUTS, CUTS[1:]):
                 nc.vector.tensor_copy(halves[t][:, a:b], planes[t][:, a:b])
             step = B if t == PACK - 1 else E - NV[t]
             for a in range(NV[t], E, step):
                 nc.scalar.activation(xb[:, a : a + step, t], listed(halves[t], a, a + step), COPY)
             nc.vector.tensor_copy(xb[:, 0 : NV[t], t], listed(planes[t], 0, NV[t]))
-
         nc.vector.tensor_copy(wb[:], w_raw[:].rearrange("p t m -> p m t"))
 
-        def quantise(a, b):
-            codes[a] = shared.tile([P, b - a], U32, name="codes%d" % a, align_bytes=64, offset=4 * a)
-            scales[a] = keep.tile([P, b - a], U8, name="scales%d" % a, align_bytes=64)
-            nc.vector.quantize_mx(
-                out=codes[a][:].bitcast(FP8X4),
-                scales=scales[a][:],
-                in_=xb[:, a:b, :].rearrange("p n t -> p (n t)"),
-            )
-
-        def multiply(acc, m, a, b):
-            nc.tensor.matmul_mx(
-                out=acc,
-                lhsT=w_codes[:, m * P : (m + 1) * P].bitcast(FP8X4),
-                lhsT_scale=w_scales[:, m * P : (m + 1) * P],
-                rhs=codes[a][:].bitcast(FP8X4),
-                rhs_scale=scales[a][:],
-                start=True,
-                stop=True,
-            )
-
         out_blocks = out.rearrange("(b p) g -> p b g", p=P)
+        n = B // K
+        banks, quantised = {}, {}
 
-        def finish(acc, blocks, a, b):
-            n = (b - a) // K
-            name = "%d_%d" % (a, blocks[0])
-            best = keep.tile([P, len(blocks), n], F32, name="best" + name)
-            res = keep.tile([P, len(blocks), n], F32, name="res" + name)
-            nc.vector.tensor_reduce(
-                out=best[:].rearrange("p b g -> p (b g)"),
-                in_=acc[:].rearrange("p (g j) -> p g j", j=K), axis=X, op=MAX,
+        def quantise(s):
+            codes = shared.tile([P, B], U32, name="codes%d" % s, align_bytes=64, offset=4 * B * (s % 2))
+            scales = keep.tile([P, B], U8, name="scales%d" % s, align_bytes=64)
+            quantised[s] = codes, scales
+            nc.vector.quantize_mx(
+                out=codes[:].bitcast(FP8X4),
+                scales=scales[:],
+                in_=xb[:, s * B : (s + 1) * B, :].rearrange("p n t -> p (n t)"),
             )
-            for i, m in enumerate(blocks):
-                nc.scalar.activation(res[:, i, :], best[:, i, :], RELU, bias=bias_sb[m][:, 0:1])
-            nc.sync.dma_start(out_blocks[:, blocks[0] : blocks[-1] + 1, a // K : b // K], res[:])
 
-        def group(a, b):
-            if b - a == 512:
-                for m in range(MB):
-                    acc = psum.tile([P, 512], F32, name="acc%d_%d" % (a, m))
-                    multiply(acc[:], m, a, b)
-                    finish(acc, [m], a, b)
+        def multiply(s, split):
+            codes, scales = quantised[s]
+            if split:
+                banks[s] = [psum.tile([P, B], F32, name="acc%d_%d" % (s, m))[:] for m in range(MB)]
+                sums = banks[s]
             else:
-                acc = psum.tile([P, 512], F32, name="acc%d" % a)
-                for m in range(MB):
-                    multiply(acc[:, m * 256 : (m + 1) * 256], m, a, b)
-                finish(acc, list(range(MB)), a, b)
+                bank = psum.tile([P, MB * B], F32, name="acc%d" % s)
+                banks[s] = [bank[:]]
+                sums = [bank[:, m * B : (m + 1) * B] for m in range(MB)]
+            for m in range(MB):
+                nc.tensor.matmul_mx(
+                    out=sums[m],
+                    lhsT=w_codes[:, m * P : (m + 1) * P].bitcast(FP8X4),
+                    lhsT_scale=w_scales[:, m * P : (m + 1) * P],
+                    rhs=codes[:].bitcast(FP8X4),
+                    rhs_scale=scales[:],
+                    start=True,
+                    stop=True,
+                )
 
-        quantise(0, 512)
+        def finish(s):
+            best = keep.tile([P, MB * n], F32, name="best%d" % s)
+            res = keep.tile([P, MB, n], F32, name="res%d" % s)
+            width = MB * n // len(banks[s])
+            for i, bank in enumerate(banks[s]):
+                nc.vector.tensor_reduce(
+                    out=best[:, i * width : (i + 1) * width],
+                    in_=bank.rearrange("p (g j) -> p g j", j=K), axis=X, op=MAX,
+                )
+            for m in range(MB):
+                nc.scalar.activation(res[:, m, :], best[:, m * n : (m + 1) * n], RELU, bias=bias_sb[m][:, 0:1])
+            nc.sync.dma_start(out_blocks[:, :, s * n : (s + 1) * n], res[:])
+
+        quantise(0)
         nc.vector.quantize_mx(
             out=w_codes[:].bitcast(FP8X4), scales=w_scales[:], in_=wb[:].rearrange("p m t -> p (m t)")
         )
-        quantise(512, 768)
-        quantise(768, 1024)
-        group(0, 512)
-        group(512, 768)
-        group(768, 1024)
+        quantise(1)
+        multiply(0, True)
+        multiply(1, False)
+        finish(0)
+        quantise(2)
+        multiply(2, False)
+        finish(1)
+        quantise(3)
+        multiply(3, True)
+        finish(2)
+        finish(3)

@@ -11,7 +11,7 @@ E = G * K
 MB = M // P
 B = 256
 CUTS = (0, 1280, T)
-NV = (384, 384, B, B)
+NV = (320, 320, B, B)
 
 F32 = mybir.dt.float32
 BF16 = mybir.dt.bfloat16
@@ -71,7 +71,17 @@ def tile_attend_edge_relu_kernel(tc, xT, w, bias, offs, out):
             for a in range(NV[t], E, step):
                 nc.scalar.activation(xb[:, a : a + step, t], listed(halves[t], a, a + step), COPY)
             nc.vector.tensor_copy(xb[:, 0 : NV[t], t], listed(planes[t], 0, NV[t]))
-        nc.vector.tensor_copy(wb[:], w_raw[:].rearrange("p t m -> p m t"))
+        for m in range(MB):
+            cols = slice(m * P, (m + 1) * P)
+            nc.vector.tensor_copy(wb[:, cols, :], w_raw[:, :, cols].rearrange("p t m -> p m t"))
+
+        def quantise_weights(m):
+            cols = slice(m * P, (m + 1) * P)
+            nc.vector.quantize_mx(
+                out=w_codes[:, cols].bitcast(FP8X4),
+                scales=w_scales[:, cols],
+                in_=wb[:, cols, :].rearrange("p m t -> p (m t)"),
+            )
 
         out_blocks = out.rearrange("(b p) g -> p b g", p=P)
         n = B // K
@@ -120,10 +130,9 @@ def tile_attend_edge_relu_kernel(tc, xT, w, bias, offs, out):
                 nc.scalar.activation(res[:, m, :], best[:, m * n : (m + 1) * n], RELU, bias=bias_sb[m][:, 0:1])
             nc.sync.dma_start(out_blocks[:, :, s * n : (s + 1) * n], res[:])
 
+        quantise_weights(0)
         quantise(0)
-        nc.vector.quantize_mx(
-            out=w_codes[:].bitcast(FP8X4), scales=w_scales[:], in_=wb[:].rearrange("p m t -> p (m t)")
-        )
+        quantise_weights(1)
         quantise(1)
         multiply(0, True)
         multiply(1, False)

@@ -11,7 +11,7 @@ E = G * K
 MB = M // P
 B = 256
 CUTS = (0, 1280, T)
-NV = (320, 320, B, B)
+NV = (352, 352, B, B)
 
 F32 = mybir.dt.float32
 BF16 = mybir.dt.bfloat16
@@ -66,14 +66,20 @@ def tile_attend_edge_relu_kernel(tc, xT, w, bias, offs, out):
 
         for t in range(PACK):
             for a, b in zip(CUTS, CUTS[1:]):
-                nc.vector.tensor_copy(halves[t][:, a:b], planes[t][:, a:b])
+                c = T - B if t == 0 and b == T else b
+                nc.vector.tensor_copy(halves[t][:, a:c], planes[t][:, a:c])
+                if c < b:
+                    nc.scalar.copy(halves[t][:, c:b], planes[t][:, c:b])
             step = B if t == PACK - 1 else E - NV[t]
             for a in range(NV[t], E, step):
                 nc.scalar.activation(xb[:, a : a + step, t], listed(halves[t], a, a + step), COPY)
             nc.vector.tensor_copy(xb[:, 0 : NV[t], t], listed(planes[t], 0, NV[t]))
         for m in range(MB):
             cols = slice(m * P, (m + 1) * P)
-            nc.vector.tensor_copy(wb[:, cols, :], w_raw[:, :, cols].rearrange("p t m -> p m t"))
+            nc.vector.tensor_copy(
+                wb[:, cols, :].rearrange("p (c i) t -> p c t i", i=4),
+                w_raw[:, :, cols].rearrange("p t (c i) -> p c t i", i=4),
+            )
 
         def quantise_weights(m):
             cols = slice(m * P, (m + 1) * P)

@@ -11,7 +11,7 @@ E = G * K
 MB = M // P
 B = 256
 CUTS = (0, 1280, T)
-NV = (352, 352, B, B)
+NV = (384, 384, B, B)
 
 F32 = mybir.dt.float32
 BF16 = mybir.dt.bfloat16
@@ -92,6 +92,7 @@ def tile_attend_edge_relu_kernel(tc, xT, w, bias, offs, out):
         out_blocks = out.rearrange("(b p) g -> p b g", p=P)
         n = B // K
         banks, quantised = {}, {}
+        results = [keep.tile([P, MB, 2 * n], F32, name="results%d" % h) for h in range(2)]
 
         def quantise(s):
             codes = shared.tile([P, B], U32, name="codes%d" % s, align_bytes=64, offset=4 * B * (s % 2))
@@ -125,7 +126,7 @@ def tile_attend_edge_relu_kernel(tc, xT, w, bias, offs, out):
 
         def finish(s):
             best = keep.tile([P, MB * n], F32, name="best%d" % s)
-            res = keep.tile([P, MB, n], F32, name="res%d" % s)
+            res = results[s // 2][:, :, (s % 2) * n : (s % 2 + 1) * n]
             width = MB * n // len(banks[s])
             for i, bank in enumerate(banks[s]):
                 nc.vector.tensor_reduce(
@@ -134,7 +135,8 @@ def tile_attend_edge_relu_kernel(tc, xT, w, bias, offs, out):
                 )
             for m in range(MB):
                 nc.scalar.activation(res[:, m, :], best[:, m * n : (m + 1) * n], RELU, bias=bias_sb[m][:, 0:1])
-            nc.sync.dma_start(out_blocks[:, :, s * n : (s + 1) * n], res[:])
+                if s % 2 == 1:
+                    nc.sync.dma_start(out_blocks[:, m, (s - 1) * n : (s + 1) * n], results[s // 2][:, m, :])
 
         quantise_weights(0)
         quantise(0)

@@ -52,10 +52,6 @@ def tile_attend_edge_relu_kernel(tc, xT, w, bias, offs, out):
             nc.sync.dma_start(b[:], bias[m * P : (m + 1) * P, :])
             bias_sb.append(b)
 
-        warm = keep.tile([P, 1], F32, name="warm")
-        nc.gpsimd.memset(warm[:], 0.0)
-        nc.scalar.activation(warm[:], warm[:], RELU)
-
         xb = keep.tile([P, E, PACK], BF16, name="xb", align_bytes=64)
         wb = keep.tile([P, M, PACK], BF16, name="wb", align_bytes=64)
         w_codes = keep.tile([P, M], U32, name="w_codes", align_bytes=64)

@@ -73,8 +73,8 @@ def tile_attend_edge_relu_kernel(tc, xT, w, bias, offs, out):
         for m in range(MB):
             cols = slice(m * P, (m + 1) * P)
             nc.vector.tensor_copy(
-                wb[:, cols, :].rearrange("p (c i) t -> p c t i", i=4),
-                w_raw[:, :, cols].rearrange("p t (c i) -> p c t i", i=4),
+                wb[:, cols, :].rearrange("p (c i) t -> p c t i", i=2),
+                w_raw[:, :, cols].rearrange("p t (c i) -> p c t i", i=2),
             )
 
         def quantise_weights(m):

@@ -11,7 +11,7 @@ E = G * K
 MB = M // P
 B = 256
 CUTS = (0, 1280, T)
-NV = (384, 384, B, B)
+NV = (352, 352, B, B)
 
 F32 = mybir.dt.float32
 BF16 = mybir.dt.bfloat16
@@ -52,7 +52,9 @@ def tile_attend_edge_relu_kernel(tc, xT, w, bias, offs, out):
             nc.sync.dma_start(b[:], bias[m * P : (m + 1) * P, :])
             bias_sb.append(b)
 
-        xb = keep.tile([P, E, PACK], BF16, name="xb", align_bytes=64)
+        xb = keep.tile([P, E - B, PACK], BF16, name="xb", align_bytes=64)
+        paired = keep.tile([P, 2, B, 2], BF16, name="paired", align_bytes=64)
+        woven = keep.tile([P, B, 2], U32, name="woven", align_bytes=64)
         wb = keep.tile([P, M, PACK], BF16, name="wb", align_bytes=64)
         w_codes = keep.tile([P, M], U32, name="w_codes", align_bytes=64)
         w_scales = keep.tile([P, M], U8, name="w_scales", align_bytes=64)
@@ -66,10 +68,14 @@ def tile_attend_edge_relu_kernel(tc, xT, w, bias, offs, out):
                 nc.vector.tensor_copy(halves[t][:, a:c], planes[t][:, a:c])
                 if c < b:
                     nc.scalar.copy(halves[t][:, c:b], planes[t][:, c:b])
-            step = B if t == PACK - 1 else E - NV[t]
-            for a in range(NV[t], E, step):
-                nc.scalar.activation(xb[:, a : a + step, t], listed(halves[t], a, a + step), COPY)
+            cut = 2 * B if t == PACK - 1 else E - B
+            nc.scalar.activation(xb[:, NV[t] : cut, t], listed(halves[t], NV[t], cut), COPY)
+            nc.scalar.activation(paired[:, t // 2, :, t % 2], listed(halves[t], E - B, E), COPY)
+            if cut < E - B:
+                nc.scalar.activation(xb[:, cut : E - B, t], listed(halves[t], cut, E - B), COPY)
             nc.vector.tensor_copy(xb[:, 0 : NV[t], t], listed(planes[t], 0, NV[t]))
+        words = paired[:].rearrange("p h n t -> p h (n t)").bitcast(U32)
+        nc.scalar.copy(woven[:], words.rearrange("p h n -> p n h"))
         for m in range(MB):
             cols = slice(m * P, (m + 1) * P)
             nc.vector.tensor_copy(
@@ -94,10 +100,14 @@ def tile_attend_edge_relu_kernel(tc, xT, w, bias, offs, out):
             codes = shared.tile([P, B], U32, name="codes%d" % s, align_bytes=64, offset=4 * B * (s % 2))
             scales = keep.tile([P, B], U8, name="scales%d" % s, align_bytes=64)
             quantised[s] = codes, scales
+            if s < 3:
+                values = xb[:, s * B : (s + 1) * B, :].rearrange("p n t -> p (n t)")
+            else:
+                values = woven[:].rearrange("p n h -> p (n h)").bitcast(BF16)
             nc.vector.quantize_mx(
                 out=codes[:].bitcast(FP8X4),
                 scales=scales[:],
-                in_=xb[:, s * B : (s + 1) * B, :].rearrange("p n t -> p (n t)"),
+                in_=values,
             )
 
         def multiply(s, split):

@@ -70,9 +70,9 @@ def tile_attend_edge_relu_kernel(tc, xT, w, bias, offs, out):
                     nc.scalar.copy(halves[t][:, c:b], planes[t][:, c:b])
             cut = 2 * B if t == PACK - 1 else E - B
             nc.scalar.activation(xb[:, NV[t] : cut, t], listed(halves[t], NV[t], cut), COPY)
-            nc.scalar.activation(paired[:, t // 2, :, t % 2], listed(halves[t], E - B, E), COPY)
             if cut < E - B:
                 nc.scalar.activation(xb[:, cut : E - B, t], listed(halves[t], cut, E - B), COPY)
+            nc.scalar.activation(paired[:, t // 2, :, t % 2], listed(halves[t], E - B, E), COPY)
             nc.vector.tensor_copy(xb[:, 0 : NV[t], t], listed(planes[t], 0, NV[t]))
         words = paired[:].rearrange("p h n t -> p h (n t)").bitcast(U32)
         nc.scalar.copy(woven[:], words.rearrange("p h n -> p n h"))
@@ -97,7 +97,7 @@ def tile_attend_edge_relu_kernel(tc, xT, w, bias, offs, out):
         results = [keep.tile([P, MB, 2 * n], F32, name="results%d" % h) for h in range(2)]
 
         def quantise(s):
-            codes = shared.tile([P, B], U32, name="codes%d" % s, align_bytes=64, offset=4 * B * (s % 2))
+            codes = shared.tile([P, B], U32, name="codes%d" % s, align_bytes=64, offset=4 * B * (0, 1, 2, 1)[s])
             scales = keep.tile([P, B], U8, name="scales%d" % s, align_bytes=64)
             quantised[s] = codes, scales
             if s < 3:
@@ -148,11 +148,11 @@ def tile_attend_edge_relu_kernel(tc, xT, w, bias, offs, out):
         quantise(0)
         quantise_weights(1)
         quantise(1)
+        quantise(2)
         multiply(0, True)
         multiply(1, False)
-        finish(0)
-        quantise(2)
         multiply(2, False)
+        finish(0)
         finish(1)
         quantise(3)
         multiply(3, True)

@@ -11,7 +11,7 @@ E = G * K
 MB = M // P
 B = 256
 CUTS = (0, 1280, T)
-NV = (352, 352, B, B)
+NV = (352, 352, 320, B)
 
 F32 = mybir.dt.float32
 BF16 = mybir.dt.bfloat16
@@ -69,13 +69,12 @@ def tile_attend_edge_relu_kernel(tc, xT, w, bias, offs, out):
                 if c < b:
                     nc.scalar.copy(halves[t][:, c:b], planes[t][:, c:b])
             cut = 2 * B if t == PACK - 1 else E - B
-            nc.scalar.activation(xb[:, NV[t] : cut, t], listed(halves[t], NV[t], cut), COPY)
-            if cut < E - B:
-                nc.scalar.activation(xb[:, cut : E - B, t], listed(halves[t], cut, E - B), COPY)
             nc.scalar.activation(paired[:, t // 2, :, t % 2], listed(halves[t], E - B, E), COPY)
+            nc.scalar.activation(xb[:, NV[t] : cut, t], listed(halves[t], NV[t], cut), COPY)
             nc.vector.tensor_copy(xb[:, 0 : NV[t], t], listed(planes[t], 0, NV[t]))
         words = paired[:].rearrange("p h n t -> p h (n t)").bitcast(U32)
         nc.scalar.copy(woven[:], words.rearrange("p h n -> p n h"))
+        nc.scalar.activation(xb[:, 2 * B : E - B, PACK - 1], listed(halves[PACK - 1], 2 * B, E - B), COPY)
         for m in range(MB):
             cols = slice(m * P, (m + 1) * P)
             nc.vector.tensor_copy(
@@ -93,11 +92,11 @@ def tile_attend_edge_relu_kernel(tc, xT, w, bias, offs, out):
 
         out_blocks = out.rearrange("(b p) g -> p b g", p=P)
         n = B // K
-        banks, quantised = {}, {}
+        banks, quantised, done = {}, {}, []
         results = [keep.tile([P, MB, 2 * n], F32, name="results%d" % h) for h in range(2)]
 
         def quantise(s):
-            codes = shared.tile([P, B], U32, name="codes%d" % s, align_bytes=64, offset=4 * B * (0, 1, 2, 1)[s])
+            codes = shared.tile([P, B], U32, name="codes%d" % s, align_bytes=64, offset=4 * B * (0, 1, 0, 2)[s])
             scales = keep.tile([P, B], U8, name="scales%d" % s, align_bytes=64)
             quantised[s] = codes, scales
             if s < 3:
@@ -133,6 +132,7 @@ def tile_attend_edge_relu_kernel(tc, xT, w, bias, offs, out):
         def finish(s):
             best = keep.tile([P, MB * n], F32, name="best%d" % s)
             res = results[s // 2][:, :, (s % 2) * n : (s % 2 + 1) * n]
+            done.append(s)
             width = MB * n // len(banks[s])
             for i, bank in enumerate(banks[s]):
                 nc.vector.tensor_reduce(
@@ -141,20 +141,20 @@ def tile_attend_edge_relu_kernel(tc, xT, w, bias, offs, out):
                 )
             for m in range(MB):
                 nc.scalar.activation(res[:, m, :], best[:, m * n : (m + 1) * n], RELU, bias=bias_sb[m][:, 0:1])
-                if s % 2 == 1:
-                    nc.sync.dma_start(out_blocks[:, m, (s - 1) * n : (s + 1) * n], results[s // 2][:, m, :])
+                if s ^ 1 in done:
+                    nc.sync.dma_start(out_blocks[:, m, s // 2 * 2 * n : (s // 2 + 1) * 2 * n], results[s // 2][:, m, :])
 
         quantise_weights(0)
         quantise(0)
         quantise_weights(1)
         quantise(1)
-        quantise(2)
+        quantise(3)
         multiply(0, True)
         multiply(1, False)
-        multiply(2, False)
+        multiply(3, False)
         finish(0)
+        quantise(2)
+        multiply(2, True)
         finish(1)
-        quantise(3)
-        multiply(3, True)
-        finish(2)
         finish(3)
+        finish(2)

@@ -11,7 +11,8 @@ E = G * K
 MB = M // P
 B = 256
 CUTS = (0, 1280, T)
-NV = (352, 352, 320, B)
+NV = (384, 352, 320, B)
+FIRST = (0, 1024, 1536, 1792, T)
 
 F32 = mybir.dt.float32
 BF16 = mybir.dt.bfloat16
@@ -38,7 +39,8 @@ def tile_attend_edge_relu_kernel(tc, xT, w, bias, offs, out):
         planes, halves = [], []
         for t in range(PACK):
             plane = keep.tile([P, T], F32, name="plane%d" % t, align_bytes=64)
-            for a, b in zip(CUTS, CUTS[1:]):
+            cuts = CUTS if t else FIRST[::2]
+            for a, b in zip(cuts, cuts[1:]):
                 nc.sync.dma_start(plane[:, a:b], x_rows[:, t, a:b])
             if t == 0:
                 nc.sync.dma_start(offsets[:], offs)
@@ -63,11 +65,12 @@ def tile_attend_edge_relu_kernel(tc, xT, w, bias, offs, out):
             return tile[:].indirect(offsets[:, a // 16 : b // 16])
 
         for t in range(PACK):
-            for a, b in zip(CUTS, CUTS[1:]):
-                c = T - B if t == 0 and b == T else b
-                nc.vector.tensor_copy(halves[t][:, a:c], planes[t][:, a:c])
-                if c < b:
-                    nc.scalar.copy(halves[t][:, c:b], planes[t][:, c:b])
+            cuts = CUTS if t else FIRST
+            for i, (a, b) in enumerate(zip(cuts, cuts[1:])):
+                if t == 0 and i % 2:
+                    nc.scalar.copy(halves[t][:, a:b], planes[t][:, a:b])
+                else:
+                    nc.vector.tensor_copy(halves[t][:, a:b], planes[t][:, a:b])
             cut = 2 * B if t == PACK - 1 else E - B
             nc.scalar.activation(paired[:, t // 2, :, t % 2], listed(halves[t], E - B, E), COPY)
             nc.scalar.activation(xb[:, NV[t] : cut, t], listed(halves[t], NV[t], cut), COPY)

@@ -11,7 +11,7 @@ E = G * K
 MB = M // P
 B = 256
 CUTS = (0, 1280, T)
-NV = (384, 352, 320, B)
+NV = (384, 352, 352, B)
 FIRST = (0, 1024, 1536, 1792, T)
 
 F32 = mybir.dt.float32
@@ -54,9 +54,7 @@ def tile_attend_edge_relu_kernel(tc, xT, w, bias, offs, out):
             nc.sync.dma_start(b[:], bias[m * P : (m + 1) * P, :])
             bias_sb.append(b)
 
-        xb = keep.tile([P, E - B, PACK], BF16, name="xb", align_bytes=64)
-        paired = keep.tile([P, 2, B, 2], BF16, name="paired", align_bytes=64)
-        woven = keep.tile([P, B, 2], U32, name="woven", align_bytes=64)
+        xb = keep.tile([P, E, PACK], BF16, name="xb", align_bytes=64)
         wb = keep.tile([P, M, PACK], BF16, name="wb", align_bytes=64)
         w_codes = keep.tile([P, M], U32, name="w_codes", align_bytes=64)
         w_scales = keep.tile([P, M], U8, name="w_scales", align_bytes=64)
@@ -71,13 +69,10 @@ def tile_attend_edge_relu_kernel(tc, xT, w, bias, offs, out):
                     nc.scalar.copy(halves[t][:, a:b], planes[t][:, a:b])
                 else:
                     nc.vector.tensor_copy(halves[t][:, a:b], planes[t][:, a:b])
-            cut = 2 * B if t == PACK - 1 else E - B
-            nc.scalar.activation(paired[:, t // 2, :, t % 2], listed(halves[t], E - B, E), COPY)
-            nc.scalar.activation(xb[:, NV[t] : cut, t], listed(halves[t], NV[t], cut), COPY)
+            ends = (B, 2 * B, 3 * B, E) if t == PACK - 1 else (NV[t], E)
+            for a, b in zip(ends, ends[1:]):
+                nc.scalar.activation(xb[:, a:b, t], listed(halves[t], a, b), COPY)
             nc.vector.tensor_copy(xb[:, 0 : NV[t], t], listed(planes[t], 0, NV[t]))
-        words = paired[:].rearrange("p h n t -> p h (n t)").bitcast(U32)
-        nc.scalar.copy(woven[:], words.rearrange("p h n -> p n h"))
-        nc.scalar.activation(xb[:, 2 * B : E - B, PACK - 1], listed(halves[PACK - 1], 2 * B, E - B), COPY)
         for m in range(MB):
             cols = slice(m * P, (m + 1) * P)
             nc.vector.tensor_copy(
@@ -99,13 +94,10 @@ def tile_attend_edge_relu_kernel(tc, xT, w, bias, offs, out):
         results = [keep.tile([P, MB, 2 * n], F32, name="results%d" % h) for h in range(2)]
 
         def quantise(s):
-            codes = shared.tile([P, B], U32, name="codes%d" % s, align_bytes=64, offset=4 * B * (0, 1, 0, 2)[s])
+            codes = shared.tile([P, B], U32, name="codes%d" % s, align_bytes=64, offset=4 * B * (0, 1, 2, 0)[s])
             scales = keep.tile([P, B], U8, name="scales%d" % s, align_bytes=64)
             quantised[s] = codes, scales
-            if s < 3:
-                values = xb[:, s * B : (s + 1) * B, :].rearrange("p n t -> p (n t)")
-            else:
-                values = woven[:].rearrange("p n h -> p (n h)").bitcast(BF16)
+            values = xb[:, s * B : (s + 1) * B, :].rearrange("p n t -> p (n t)")
             nc.vector.quantize_mx(
                 out=codes[:].bitcast(FP8X4),
                 scales=scales[:],
@@ -151,13 +143,13 @@ def tile_attend_edge_relu_kernel(tc, xT, w, bias, offs, out):
         quantise(0)
         quantise_weights(1)
         quantise(1)
-        quantise(3)
+        quantise(2)
         multiply(0, True)
         multiply(1, False)
-        multiply(3, False)
+        multiply(2, False)
         finish(0)
-        quantise(2)
-        multiply(2, True)
+        quantise(3)
+        multiply(3, True)
         finish(1)
-        finish(3)
         finish(2)
+        finish(3)

@@ -91,7 +91,7 @@ def tile_attend_edge_relu_kernel(tc, xT, w, bias, offs, out):
         out_blocks = out.rearrange("(b p) g -> p b g", p=P)
         n = B // K
         banks, quantised, done = {}, {}, []
-        results = [keep.tile([P, MB, 2 * n], F32, name="results%d" % h) for h in range(2)]
+        results = {}
 
         def quantise(s):
             codes = shared.tile([P, B], U32, name="codes%d" % s, align_bytes=64, offset=4 * B * (0, 1, 2, 0)[s])
@@ -124,20 +124,27 @@ def tile_attend_edge_relu_kernel(tc, xT, w, bias, offs, out):
                     stop=True,
                 )
 
-        def finish(s):
+        def largest(dst, src):
+            nc.vector.tensor_reduce(out=dst, in_=src.rearrange("p (g j) -> p g j", j=K), axis=X, op=MAX)
+
+        def place(s, m):
+            return results[s // 2][:, m, (s % 2) * n : (s % 2 + 1) * n]
+
+        def stored(s, m):
+            done.append((s, m))
+            if (s ^ 1, m) in done:
+                nc.sync.dma_start(out_blocks[:, m, s // 2 * 2 * n : (s // 2 + 1) * 2 * n], results[s // 2][:, m, :])
+
+        def finish(s, blocks=(0, 1)):
             best = keep.tile([P, MB * n], F32, name="best%d" % s)
-            res = results[s // 2][:, :, (s % 2) * n : (s % 2 + 1) * n]
-            done.append(s)
-            width = MB * n // len(banks[s])
-            for i, bank in enumerate(banks[s]):
-                nc.vector.tensor_reduce(
-                    out=best[:, i * width : (i + 1) * width],
-                    in_=bank.rearrange("p (g j) -> p g j", j=K), axis=X, op=MAX,
-                )
-            for m in range(MB):
-                nc.scalar.activation(res[:, m, :], best[:, m * n : (m + 1) * n], RELU, bias=bias_sb[m][:, 0:1])
-                if s ^ 1 in done:
-                    nc.sync.dma_start(out_blocks[:, m, s // 2 * 2 * n : (s // 2 + 1) * 2 * n], results[s // 2][:, m, :])
+            if len(banks[s]) == 1:
+                largest(best[:], banks[s][0])
+            else:
+                for m in blocks:
+                    largest(best[:, m * n : (m + 1) * n], banks[s][m])
+            for m in blocks:
+                nc.scalar.activation(place(s, m), best[:, m * n : (m + 1) * n], RELU, bias=bias_sb[m][:, 0:1])
+                stored(s, m)
 
         quantise_weights(0)
         quantise(0)
@@ -146,10 +153,16 @@ def tile_attend_edge_relu_kernel(tc, xT, w, bias, offs, out):
         quantise(2)
         multiply(0, True)
         multiply(1, False)
-        multiply(2, False)
+        multiply(2, True)
+        results[0] = keep.tile([P, MB, 2 * n], F32, name="results0")
         finish(0)
         quantise(3)
         multiply(3, True)
+        results[1] = shared.tile([P, MB, 2 * n], F32, name="results1", align_bytes=64, offset=0)
         finish(1)
-        finish(2)
+        clamped = keep.tile([P, B], F32, name="clamped")
+        nc.scalar.activation(clamped[:], banks[2][1], RELU, bias=bias_sb[1][:, 0:1])
+        finish(2, (0,))
         finish(3)
+        largest(place(2, 1), clamped[:])
+        stored(2, 1)

@@ -10,7 +10,7 @@ PACK = 4
 E = G * K
 MB = M // P
 B = 256
-CUTS = (0, 1280, T)
+CUTS = (0, 1408, T)
 NV = (384, 352, 352, B)
 FIRST = (0, 1024, 1536, 1792, T)
 

@@ -11,7 +11,8 @@ E = G * K
 MB = M // P
 B = 256
 CUTS = (0, 1408, T)
-NV = (384, 352, 352, B)
+NV = (448, 320, 352, B)
+SECOND = (0, 1408, 1856, T)
 FIRST = (0, 1024, 1536, 1792, T)
 
 F32 = mybir.dt.float32
@@ -63,9 +64,9 @@ def tile_attend_edge_relu_kernel(tc, xT, w, bias, offs, out):
             return tile[:].indirect(offsets[:, a // 16 : b // 16])
 
         for t in range(PACK):
-            cuts = CUTS if t else FIRST
+            cuts = (FIRST, SECOND, CUTS, CUTS)[t]
             for i, (a, b) in enumerate(zip(cuts, cuts[1:])):
-                if t == 0 and i % 2:
+                if (t == 0 and i % 2) or (t == 1 and i == 2):
                     nc.scalar.copy(halves[t][:, a:b], planes[t][:, a:b])
                 else:
                     nc.vector.tensor_copy(halves[t][:, a:b], planes[t][:, a:b])

from contextlib import ExitStack

import concourse.mybir as mybir

G, K, T, D, M = 256, 4, 2048, 512, 256
FLOPS = 2 * D * M * G * K

P = 128
PACK = 4
E = G * K
MB = M // P
B = 256
CUTS = (0, 1408, T)
NV = (448, 320, 352, B)
SECOND = (0, 1408, 1856, T)
FIRST = (0, 1024, 1536, 1792, T)

F32 = mybir.dt.float32
BF16 = mybir.dt.bfloat16
U32 = mybir.dt.uint32
U16 = mybir.dt.uint16
U8 = mybir.dt.uint8
FP8X4 = mybir.dt.float8_e4m3fn_x4
MAX = mybir.AluOpType.max
RELU = mybir.ActivationFunctionType.Relu
COPY = mybir.ActivationFunctionType.Copy
X = mybir.AxisListType.X


def tile_attend_edge_relu_kernel(tc, xT, w, bias, offs, out):
    nc = tc.nc
    with ExitStack() as ctx:
        keep = ctx.enter_context(tc.tile_pool(name="keep", bufs=1))
        shared = ctx.enter_context(tc.tile_pool(name="shared", bufs=1))
        psum = ctx.enter_context(tc.psum_pool(name="psum", bufs=1))

        offsets = keep.tile([P, E // 16], U16, name="offsets")

        x_rows = xT.rearrange("(p t) c -> p t c", t=PACK)
        planes, halves = [], []
        for t in range(PACK):
            plane = keep.tile([P, T], F32, name="plane%d" % t, align_bytes=64)
            cuts = CUTS if t else FIRST[::2]
            for a, b in zip(cuts, cuts[1:]):
                nc.sync.dma_start(plane[:, a:b], x_rows[:, t, a:b])
            if t == 0:
                nc.sync.dma_start(offsets[:], offs)
            planes.append(plane)
            halves.append(keep.tile([P, T], BF16, name="half%d" % t, align_bytes=64))
        w_raw = shared.tile([P, PACK, M], F32, name="w_raw", align_bytes=64, offset=0)
        nc.sync.dma_start(w_raw[:], w.rearrange("(p t) m -> p t m", t=PACK))
        bias_sb = []
        for m in range(MB):
            b = keep.tile([P, 1], F32, name="bias%d" % m)
            nc.sync.dma_start(b[:], bias[m * P : (m + 1) * P, :])
            bias_sb.append(b)

        xb = keep.tile([P, E, PACK], BF16, name="xb", align_bytes=64)
        wb = keep.tile([P, M, PACK], BF16, name="wb", align_bytes=64)
        w_codes = keep.tile([P, M], U32, name="w_codes", align_bytes=64)
        w_scales = keep.tile([P, M], U8, name="w_scales", align_bytes=64)

        def listed(tile, a, b):
            return tile[:].indirect(offsets[:, a // 16 : b // 16])

        for t in range(PACK):
            cuts = (FIRST, SECOND, CUTS, CUTS)[t]
            for i, (a, b) in enumerate(zip(cuts, cuts[1:])):
                if (t == 0 and i % 2) or (t == 1 and i == 2):
                    nc.scalar.copy(halves[t][:, a:b], planes[t][:, a:b])
                else:
                    nc.vector.tensor_copy(halves[t][:, a:b], planes[t][:, a:b])
            ends = (B, 2 * B, 3 * B, E) if t == PACK - 1 else (NV[t], E)
            for a, b in zip(ends, ends[1:]):
                nc.scalar.activation(xb[:, a:b, t], listed(halves[t], a, b), COPY)
            nc.vector.tensor_copy(xb[:, 0 : NV[t], t], listed(planes[t], 0, NV[t]))
        for m in range(MB):
            cols = slice(m * P, (m + 1) * P)
            nc.vector.tensor_copy(
                wb[:, cols, :].rearrange("p (c i) t -> p c t i", i=2),
                w_raw[:, :, cols].rearrange("p t (c i) -> p c t i", i=2),
            )

        def quantise_weights(m):
            cols = slice(m * P, (m + 1) * P)
            nc.vector.quantize_mx(
                out=w_codes[:, cols].bitcast(FP8X4),
                scales=w_scales[:, cols],
                in_=wb[:, cols, :].rearrange("p m t -> p (m t)"),
            )

        out_blocks = out.rearrange("(b p) g -> p b g", p=P)
        n = B // K
        banks, quantised, done = {}, {}, []
        results = {}

        def quantise(s):
            codes = shared.tile([P, B], U32, name="codes%d" % s, align_bytes=64, offset=4 * B * (0, 1, 2, 0)[s])
            scales = keep.tile([P, B], U8, name="scales%d" % s, align_bytes=64)
            quantised[s] = codes, scales
            values = xb[:, s * B : (s + 1) * B, :].rearrange("p n t -> p (n t)")
            nc.vector.quantize_mx(
                out=codes[:].bitcast(FP8X4),
                scales=scales[:],
                in_=values,
            )

        def multiply(s, split):
            codes, scales = quantised[s]
            if split:
                banks[s] = [psum.tile([P, B], F32, name="acc%d_%d" % (s, m))[:] for m in range(MB)]
                sums = banks[s]
            else:
                bank = psum.tile([P, MB * B], F32, name="acc%d" % s)
                banks[s] = [bank[:]]
                sums = [bank[:, m * B : (m + 1) * B] for m in range(MB)]
            for m in range(MB):
                nc.tensor.matmul_mx(
                    out=sums[m],
                    lhsT=w_codes[:, m * P : (m + 1) * P].bitcast(FP8X4),
                    lhsT_scale=w_scales[:, m * P : (m + 1) * P],
                    rhs=codes[:].bitcast(FP8X4),
                    rhs_scale=scales[:],
                    start=True,
                    stop=True,
                )

        def largest(dst, src):
            nc.vector.tensor_reduce(out=dst, in_=src.rearrange("p (g j) -> p g j", j=K), axis=X, op=MAX)

        def place(s, m):
            return results[s // 2][:, m, (s % 2) * n : (s % 2 + 1) * n]

        def stored(s, m):
            done.append((s, m))
            if (s ^ 1, m) in done:
                nc.sync.dma_start(out_blocks[:, m, s // 2 * 2 * n : (s // 2 + 1) * 2 * n], results[s // 2][:, m, :])

        def finish(s, blocks=(0, 1)):
            best = keep.tile([P, MB * n], F32, name="best%d" % s)
            if len(banks[s]) == 1:
                largest(best[:], banks[s][0])
            else:
                for m in blocks:
                    largest(best[:, m * n : (m + 1) * n], banks[s][m])
            for m in blocks:
                nc.scalar.activation(place(s, m), best[:, m * n : (m + 1) * n], RELU, bias=bias_sb[m][:, 0:1])
                stored(s, m)

        quantise_weights(0)
        quantise(0)
        quantise_weights(1)
        quantise(1)
        quantise(2)
        multiply(0, True)
        multiply(1, False)
        multiply(2, True)
        results[0] = keep.tile([P, MB, 2 * n], F32, name="results0")
        finish(0)
        quantise(3)
        multiply(3, True)
        results[1] = shared.tile([P, MB, 2 * n], F32, name="results1", align_bytes=64, offset=0)
        finish(1)
        clamped = keep.tile([P, B], F32, name="clamped")
        nc.scalar.activation(clamped[:], banks[2][1], RELU, bias=bias_sb[1][:, 0:1])
        finish(2, (0,))
        finish(3)
        largest(place(2, 1), clamped[:])
        stored(2, 1)
